import numpy as np
import ml_dtypes


def mxq(x, axis, fmt="e4m3"):
    dtype, down = {"e4m3": (ml_dtypes.float8_e4m3fn, 7), "e5m2": (ml_dtypes.float8_e5m2, 14)}[fmt]
    v = np.moveaxis(np.asarray(x, np.float32).astype(ml_dtypes.bfloat16).astype(np.float64), axis, -1)
    blocks = v.reshape(v.shape[:-1] + (-1, 32))
    amax = np.abs(blocks).max(-1, keepdims=True)
    byte = np.maximum(np.where(amax > 0, np.frexp(amax)[1] - 1 + 127, 0) - down, 1)
    scale = np.exp2(byte - 127.0)
    codes = (blocks / scale).astype(np.float32).astype(dtype).astype(np.float64)
    return np.moveaxis((codes * scale).reshape(v.shape), -1, axis)


WIDE = False


def mx_kscale(k):
    if not WIDE:
        return np.ones(k)
    levels = np.array([10, -10, 5, -5, 0])
    if k % 512:
        return np.exp2(np.random.permutation(np.resize(levels, k // 32))).repeat(32)
    a = np.empty((k // 512, 16))
    for p in range(k // 512):
        a[p, :8] = np.random.permutation(np.resize(levels, 8))
        for g in range(8):
            far = levels[np.abs(levels - a[p, g]) >= 10]
            a[p, g + 8] = far[np.random.randint(len(far))]
    return np.exp2(a.ravel()).repeat(32)


def f64(x):
    return np.asarray(x).astype(np.float64)


def striped(idx):
    return np.tile(np.asarray(idx).reshape(-1, 16).T, (8, 1)).astype(np.uint16)


def unstriped(offs):
    return offs[:16].T.reshape(-1).astype(np.int64)


def striped8(idx):
    return np.asarray(idx).reshape(8, -1, 16).transpose(0, 2, 1).reshape(128, -1).astype(np.uint16)


def unstriped8(offs):
    return offs.reshape(8, 16, -1).transpose(0, 2, 1).reshape(8, -1).astype(np.int64)


def pick8(x, idx, run):
    r = np.arange(len(x))
    return x[r[:, None], idx[r % (8 * run) // run]]


E2M1 = np.array([0.0, 0.5, 1.0, 1.5, 2.0, 3.0, 4.0, 6.0, -0.0, -0.5, -1.0, -1.5, -2.0, -3.0, -4.0, -6.0])


def pack_weight(w, fmt):
    k, n = w.shape
    w = f64(np.asarray(w, np.float32).astype(ml_dtypes.bfloat16)).reshape(k // 32, 32, n)
    amax = np.abs(w).max(1)
    if fmt == "e4m3":
        byte = np.frexp(amax)[1] - 1 + 127 - 7
    else:
        mant, ex = np.frexp(amax / 6.0)
        byte = np.where(mant > 0.5, ex, ex - 1) + 127
    byte = np.clip(np.where(amax > 0, byte, 1), 1, 254)
    scaled = (w * np.exp2(127.0 - byte)[:, None, :]).reshape(k, n).astype(np.float32)
    by_word = np.ascontiguousarray(scaled.reshape(k // 512, 128, 4, n).transpose(0, 1, 3, 2))
    if fmt == "e4m3":
        words = by_word.astype(ml_dtypes.float8_e4m3fn).view(np.uint8)
    else:
        c = by_word.astype(ml_dtypes.float4_e2m1fn).view(np.uint8) & 0xF
        words = (c[..., 0::2] | (c[..., 1::2] << 4)).reshape(k // 512, 128, 2 * n)
    return np.ascontiguousarray(words), np.ascontiguousarray(byte.astype(np.uint8).reshape(k // 512, 16, n))


def unpack_weight(words, scales, fmt):
    g, _, n = scales.shape
    words = np.ascontiguousarray(words).reshape(g, 128, n, -1)
    if fmt == "e4m3":
        vals = words.view(ml_dtypes.float8_e4m3fn).astype(np.float64)
    else:
        nib = np.empty((g, 128, n, 4), np.uint8)
        nib[..., 0::2] = words & 0xF
        nib[..., 1::2] = words >> 4
        vals = E2M1[nib]
    vals = vals * np.repeat(np.exp2(scales.astype(np.float64) - 127.0), 8, axis=1)[..., None]
    return vals.transpose(0, 1, 3, 2).reshape(g * 512, n)


def sgn(shape):
    return np.random.uniform(0.5, 2.0, shape) * np.where(np.random.standard_normal(shape) < 0, -1.0, 1.0)


K, J, R, T, U, Z, M, S, O, N, G = 512, 512, 512, 2048, 2048, 512, 1024, 256, 128, 256, 256


def setup_inputs():
    n = np.random.standard_normal
    idx = np.stack([np.random.permutation(T)[:J] for _ in range(8)])
    idx2 = np.stack([np.random.permutation(U)[:J] for _ in range(8)])
    idx3 = np.random.permutation(M)[:J]
    idx4 = np.stack([np.random.permutation(J)[:S] for _ in range(8)])
    idx5 = np.random.permutation(J)[:S]
    idx6 = np.stack([np.random.permutation(G)[:O] for _ in range(8)])
    idx7 = np.stack([np.random.permutation(G)[:O] for _ in range(8)])
    fk = mx_kscale(K)
    fr = mx_kscale(R)
    fz = mx_kscale(Z)
    wp = pack_weight(n((K, R)) * 1 / np.sqrt(K) / fk[:, None] * fr, "e2m1")
    xop = pack_weight(n((Z, M)) / fz[:, None], "e2m1")
    w2p = pack_weight(n((Z, R)) * 1 / np.sqrt(Z) * fz[:, None] * fr, "e4m3")
    wbp = pack_weight(n((R, N)) * 1 / np.sqrt(R) / fr[:, None], "e4m3")
    return {
        "ta": (np.random.randint(-7, 8, (K, T)).astype(np.float64)).astype(np.float32),
        "tb": (np.random.randint(-7, 8, (K, U)).astype(np.float64)).astype(np.float32),
        "ga": ((np.random.randint(8, 25, (K, 1)) / 64.0) * fk[:, None]).astype(np.float32),
        "gb": ((np.random.randint(8, 25, (K, 1)) / 64.0) * fk[:, None]).astype(np.float32),
        "w_words": wp[0],
        "w_scales": wp[1],
        "xo_words": xop[0],
        "xo_scales": xop[1],
        "w2_words": w2p[0],
        "w2_scales": w2p[1],
        "sa": (sgn((R, 1))).astype(np.float32),
        "sb": (sgn((R, 1))).astype(np.float32),
        "wb_words": wbp[0],
        "wb_scales": wbp[1],
        "tz": (np.random.randint(-7, 8, (N, G)).astype(np.float64)).astype(np.float32),
        "so": (np.random.randint(8, 25, (N, 1)) / 64.0).astype(np.float32),
        "sp": (np.random.randint(4, 15, (N, 1)) / 64.0).astype(np.float32),
        "offs": striped8(idx),
        "offs2": striped8(idx2),
        "offs3": striped(idx3),
        "offs4": striped8(idx4),
        "offs5": striped(idx5),
        "offs6": striped8(idx6),
        "offs7": striped8(idx7),
    }


def reference(ta, tb, ga, gb, w_words, w_scales, xo_words, xo_scales, w2_words, w2_scales, sa, sb, wb_words, wb_scales, tz, so, sp, offs, offs2, offs3, offs4, offs5, offs6, offs7):
    idx = unstriped8(offs)
    idx2 = unstriped8(offs2)
    idx3 = unstriped(offs3)
    idx4 = unstriped8(offs4)
    idx5 = unstriped(offs5)
    idx6 = unstriped8(offs6)
    idx7 = unstriped8(offs7)
    wu = unpack_weight(w_words, w_scales, "e2m1")
    xou = unpack_weight(xo_words, xo_scales, "e2m1")
    w2u = unpack_weight(w2_words, w2_scales, "e4m3")
    wbu = unpack_weight(wb_words, wb_scales, "e4m3")
    xc = np.maximum(pick8(f64(ta), idx, 64) * f64(ga), pick8(f64(tb), idx2, 64) * f64(gb))
    xcq = mxq(xc, 0, "e4m3")
    xoidx3g = xou[:, idx3]
    a = wu.T @ xcq + w2u.T @ xoidx3g
    h1 = np.maximum(pick8(a, idx4, 64) * f64(sa), a[:, idx5] * f64(sb))
    hid = h1.reshape(R, O, S // O).max(axis=2)
    hidq = mxq(hid, 0, "e4m3")
    p = wbu.T @ hidq
    y = np.maximum(np.minimum(p, pick8(f64(tz), idx6, 16) * f64(so)), pick8(f64(tz), idx7, 16) * f64(sp))
    return y

@@ -1,0 +1,198 @@
+from contextlib import ExitStack
+
+import concourse.mybir as mybir
+
+K, J, R, T, M, S, O, N, G = 512, 512, 512, 2048, 1024, 256, 128, 256, 256
+FLOPS = 2 * (2 * K * R * J + R * N * O)
+
+F32 = mybir.dt.float32
+BF16 = mybir.dt.bfloat16
+I32 = mybir.dt.int32
+U32 = mybir.dt.uint32
+U16 = mybir.dt.uint16
+U8 = mybir.dt.uint8
+FP8X4 = mybir.dt.float8_e4m3fn_x4
+FP4X4 = mybir.dt.float4_e2m1fn_x4
+COPY = mybir.ActivationFunctionType.Copy
+MAX = mybir.AluOpType.max
+MIN = mybir.AluOpType.min
+XY = mybir.AxisListType.XY
+
+P = 128
+PACK = 4
+HALF = J // 2
+
+
+def tile_picked_largercode_plain_bank_pooledgroups_one_lastbounds_kernel(tc, ta, tb, ga, gb, w_words, w_scales, xo_words, xo_scales, w2_words, w2_scales,
+        sa, sb, wb_words, wb_scales, tz, so, sp, offs, offs2, offs3, offs4, offs5, offs6, offs7, out):
+    nc = tc.nc
+    with ExitStack() as ctx:
+        keep = ctx.enter_context(tc.tile_pool(name="keep", bufs=1))
+        psum = ctx.enter_context(tc.psum_pool(name="psum", bufs=1))
+
+        def sb_tile(shape, dtype, name):
+            return keep.tile(shape, dtype, name=name, align_bytes=64)
+
+        def load(shape, dtype, name, src):
+            t = sb_tile(shape, dtype, name)
+            nc.sync.dma_start(out=t[:], in_=src)
+            return t
+
+        def load_table(src, t, name):
+            return load([P, T], F32, name + str(t), src.rearrange("(p t) c -> t p c", t=PACK)[t])
+
+        def load_list(src, name):
+            return load(list(src.shape), U16, name, src)
+
+        def load_factor(src, name):
+            return load([P, PACK], F32, name, src.rearrange("(p t) o -> p (t o)", t=PACK))
+
+        def load_bound_step(src, name):
+            t = sb_tile([P, N // P], F32, name)
+            with nc.allow_non_contiguous_dma(reason="one value a partition and block"):
+                nc.sync.dma_start(out=t[:], in_=src.rearrange("(b p) o -> p (b o)", p=P))
+            return t
+
+        def load_words(src, nbytes, name):
+            t = sb_tile([P, nbytes], U8, name)
+            nc.sync.dma_start(out=t[:].bitcast(I32), in_=src.bitcast(I32))
+            return t
+
+        def stage_scales(src, cols, name):
+            t = sb_tile([P, 2, cols], U8, name)
+            for u in range(2):
+                nc.sync.dma_start(out=t[64 * u:64 * u + 4].bitcast(I32),
+                                  in_=src[0, 8 * u:8 * u + 8, :].rearrange("(q i) c -> i q c", i=4).bitcast(I32))
+            return t
+
+        def spread_scales(stage, cols, name):
+            plane = sb_tile([P, cols], U8, name)
+            nc.vector.memset(plane[:].bitcast(I32), 0)
+            for quad in range(4):
+                u, q = divmod(quad, 2)
+                nc.vector.tensor_copy(out=plane[32 * quad:32 * quad + 4, :].bitcast(I32),
+                                      in_=stage[64 * u:64 * u + 4, q, :].bitcast(I32))
+            return plane
+
+        def deal_scales(plane, name):
+            dealt = sb_tile([P, R], U8, name)
+            nc.vector.tensor_copy(out=dealt[:].rearrange("p (t m) -> p t m", t=PACK),
+                                  in_=plane[:].rearrange("p (m t) -> p t m", t=PACK))
+            return dealt
+
+        tas, tbs = [], []
+        tas.append(load_table(ta, 0, "ta"))
+        l1 = load_list(offs, "l1")
+        ga_t = load_factor(ga, "ga_t")
+        tbs.append(load_table(tb, 0, "tb"))
+        l2 = load_list(offs2, "l2")
+        gb_t = load_factor(gb, "gb_t")
+        tas.append(load_table(ta, 1, "ta"))
+        l3 = load_list(offs3, "l3")
+        xo_w = load_words(xo_words[0], 2 * M, "xo_w")
+        xo_st = stage_scales(xo_scales, M, "xo_st")
+        tbs.append(load_table(tb, 1, "tb"))
+        w_w = load_words(w_words[0], 2 * R, "w_w")
+        w_st = stage_scales(w_scales, R, "w_st")
+        w2_w = load_words(w2_words[0].rearrange("p c t -> p (c t)"), 4 * R, "w2_w")
+        w2_st = stage_scales(w2_scales, R, "w2_st")
+        for t in (2, 3):
+            tas.append(load_table(ta, t, "ta"))
+            tbs.append(load_table(tb, t, "tb"))
+        tzs = [load([P, G], F32, "tz0", tz[0:P, :])]
+        l6 = load_list(offs6, "l6")
+        so_t = load_bound_step(so, "so_t")
+        l7 = load_list(offs7, "l7")
+        sp_t = load_bound_step(sp, "sp_t")
+        tzs.append(load([P, G], F32, "tz1", tz[P:2 * P, :]))
+        l4 = load_list(offs4, "l4")
+        sa_t = load_factor(sa, "sa_t")
+        l5 = load_list(offs5, "l5")
+        sb_t = load_factor(sb, "sb_t")
+        wb_w = load_words(wb_words[0].rearrange("p c t -> p (c t)"), 4 * N, "wb_w")
+        wb_st = stage_scales(wb_scales, N, "wb_st")
+
+        xo_s = spread_scales(xo_st, M, "xo_s")
+        xg_w = sb_tile([P, 2 * J], U8, "xg_w")
+        xg_s = sb_tile([P, J], U8, "xg_s")
+        nc.vector.tensor_copy(out=xg_w[:].bitcast(U16), in_=xo_w[:].bitcast(U16).indirect(l3[:]))
+        nc.vector.tensor_copy(out=xg_s[:], in_=xo_s[:].indirect(l3[:]))
+
+        wd_w = sb_tile([P, 2 * R], U8, "wd_w")
+        nc.scalar.copy(out=wd_w[:].bitcast(U16).rearrange("p (t m) -> p t m", t=PACK),
+                       in_=w_w[:].bitcast(U16).rearrange("p (m t) -> p t m", t=PACK))
+        wd_s = deal_scales(spread_scales(w_st, R, "w_s"), "wd_s")
+        w2d_w = sb_tile([P, 4 * R], U8, "w2d_w")
+        nc.vector.tensor_copy(out=w2d_w[:].bitcast(I32).rearrange("p (t m) -> p t m", t=PACK),
+                              in_=w2_w[:].bitcast(I32).rearrange("p (m t) -> p t m", t=PACK))
+        w2d_s = deal_scales(spread_scales(w2_st, R, "w2_s"), "w2d_s")
+
+        groups = [(0, 0, HALF), (0, HALF, HALF)] + [(t, 0, J) for t in range(1, PACK)]
+        banks = [psum.tile([P, width], F32, name="acc%d" % i) for i, (t, c0, width) in enumerate(groups)]
+        for bank, (t, c0, width) in zip(banks, groups):
+            nc.tensor.matmul_mx(out=bank[:],
+                                lhsT=w2d_w[:, 4 * P * t:4 * P * (t + 1)].bitcast(FP8X4),
+                                lhsT_scale=w2d_s[:, P * t:P * (t + 1)],
+                                rhs=xg_w[:, 2 * c0:2 * (c0 + width)].bitcast(FP4X4),
+                                rhs_scale=xg_s[:, c0:c0 + width], start=True, stop=False)
+
+        xcs = [sb_tile([P, HALF, PACK], BF16, "xc%d" % h) for h in range(2)]
+        xq_w = sb_tile([P, J], U32, "xq_w")
+        xq_s = sb_tile([P, J], U8, "xq_s")
+        for t in range(PACK):
+            pa = sb_tile([P, J], F32, "pa%d" % t)
+            pb = sb_tile([P, J], F32, "pb%d" % t)
+            nc.scalar.activation(out=pa[:], in_=tas[t][:].indirect(l1[:]), func=COPY, scale=ga_t[:, t:t + 1])
+            nc.scalar.activation(out=pb[:], in_=tbs[t][:].indirect(l2[:]), func=COPY, scale=gb_t[:, t:t + 1])
+            for h in range(2):
+                cols = slice(HALF * h, HALF * (h + 1))
+                nc.vector.tensor_tensor(out=xcs[h][:, :, t], in0=pa[:, cols], in1=pb[:, cols], op=MAX)
+        for h in range(2):
+            cols = slice(HALF * h, HALF * (h + 1))
+            nc.vector.quantize_mx(out=xq_w[:, cols].bitcast(FP8X4), scales=xq_s[:, cols],
+                                  in_=xcs[h][:].rearrange("p j t -> p (j t)"))
+
+        upper = sb_tile([P, N // P, O], F32, "upper")
+        lower = sb_tile([P, N // P, O], F32, "lower")
+        for b in range(N // P):
+            nc.scalar.activation(out=upper[:, b, :], in_=tzs[b][:].indirect(l6[:]), func=COPY, scale=so_t[:, b:b + 1])
+            nc.scalar.activation(out=lower[:, b, :], in_=tzs[b][:].indirect(l7[:]), func=COPY, scale=sp_t[:, b:b + 1])
+
+        hidden = [sb_tile([P, J], F32, "hidden%d" % t) for t in range(PACK)]
+        for i, (bank, (t, c0, width)) in enumerate(zip(banks, groups)):
+            nc.tensor.matmul_mx(out=bank[:],
+                                lhsT=wd_w[:, 2 * P * t:2 * P * (t + 1)].bitcast(FP4X4),
+                                lhsT_scale=wd_s[:, P * t:P * (t + 1)],
+                                rhs=xq_w[:, c0:c0 + width].bitcast(FP8X4),
+                                rhs_scale=xq_s[:, c0:c0 + width], start=False, stop=True)
+            if i == 0:
+                nc.scalar.copy(out=hidden[t][:, c0:c0 + width], in_=bank[:])
+            else:
+                nc.vector.tensor_copy(out=hidden[t][:, c0:c0 + width], in_=bank[:])
+
+        wb_s = spread_scales(wb_st, N, "wb_s")
+
+        hid = sb_tile([P, O, PACK], BF16, "hid")
+        for t in range(PACK):
+            picks = sb_tile([P, 2, S], F32, "picks%d" % t)
+            nc.scalar.activation(out=picks[:, 0, :], in_=hidden[t][:].indirect(l4[:]), func=COPY, scale=sa_t[:, t:t + 1])
+            nc.scalar.activation(out=picks[:, 1, :], in_=hidden[t][:].indirect(l5[:]), func=COPY, scale=sb_t[:, t:t + 1])
+            nc.vector.tensor_reduce(out=hid[:, :, t], in_=picks[:].rearrange("p u (o e) -> p o u e", e=2), axis=XY, op=MAX)
+
+        hq_w = sb_tile([P, O], U32, "hq_w")
+        hq_s = sb_tile([P, O], U8, "hq_s")
+        nc.vector.quantize_mx(out=hq_w[:].bitcast(FP8X4), scales=hq_s[:], in_=hid[:].rearrange("p o t -> p (o t)"))
+
+        prods = [psum.tile([P, O], F32, name="prod%d" % b) for b in range(N // P)]
+        capped = [sb_tile([P, O], F32, "capped%d" % b) for b in range(N // P)]
+        result = [sb_tile([P, O], F32, "result%d" % b) for b in range(N // P)]
+        for b in range(N // P):
+            nc.tensor.matmul_mx(out=prods[b][:],
+                                lhsT=wb_w[:, 4 * P * b:4 * P * (b + 1)].bitcast(FP8X4),
+                                lhsT_scale=wb_s[:, P * b:P * (b + 1)],
+                                rhs=hq_w[:].bitcast(FP8X4), rhs_scale=hq_s[:], start=True, stop=True)
+        for b in range(N // P):
+            nc.vector.tensor_tensor(out=capped[b][:], in0=prods[b][:], in1=upper[:, b, :], op=MIN)
+        for b in range(N // P):
+            nc.vector.tensor_tensor(out=result[b][:], in0=capped[b][:], in1=lower[:, b, :], op=MAX)
+            nc.sync.dma_start(out=out[P * b:P * (b + 1), :], in_=result[b][:])

@@ -20,7 +20,10 @@ XY = mybir.AxisListType.XY
 
 P = 128
 PACK = 4
-HALF = J // 2
+CHUNK = 128
+CHUNKS = J // CHUNK
+ON_SCALAR = 2
+POOLS = O // 2
 
 
 def tile_picked_largercode_plain_bank_pooledgroups_one_lastbounds_kernel(tc, ta, tb, ga, gb, w_words, w_scales, xo_words, xo_scales, w2_words, w2_scales,
@@ -76,10 +79,13 @@ def tile_picked_largercode_plain_bank_pooledgroups_one_lastbounds_kernel(tc, ta,
 
         def deal_scales(plane, name):
             dealt = sb_tile([P, R], U8, name)
-            nc.vector.tensor_copy(out=dealt[:].rearrange("p (t m) -> p t m", t=PACK),
-                                  in_=plane[:].rearrange("p (m t) -> p t m", t=PACK))
+            nc.vector.tensor_copy(out=dealt[:].rearrange("p (t m) -> p m t", t=PACK),
+                                  in_=plane[:].rearrange("p (m t) -> p m t", t=PACK))
             return dealt
 
+        xo_st = stage_scales(xo_scales, M, "xo_st")
+        w2_st = stage_scales(w2_scales, R, "w2_st")
+        w_st = stage_scales(w_scales, R, "w_st")
         tas, tbs = [], []
         tas.append(load_table(ta, 0, "ta"))
         l1 = load_list(offs, "l1")
@@ -90,27 +96,27 @@ def tile_picked_largercode_plain_bank_pooledgroups_one_lastbounds_kernel(tc, ta,
         tas.append(load_table(ta, 1, "ta"))
         l3 = load_list(offs3, "l3")
         xo_w = load_words(xo_words[0], 2 * M, "xo_w")
-        xo_st = stage_scales(xo_scales, M, "xo_st")
         tbs.append(load_table(tb, 1, "tb"))
-        w_w = load_words(w_words[0], 2 * R, "w_w")
-        w_st = stage_scales(w_scales, R, "w_st")
-        w2_w = load_words(w2_words[0].rearrange("p c t -> p (c t)"), 4 * R, "w2_w")
-        w2_st = stage_scales(w2_scales, R, "w2_st")
         for t in (2, 3):
             tas.append(load_table(ta, t, "ta"))
             tbs.append(load_table(tb, t, "tb"))
-        tzs = [load([P, G], F32, "tz0", tz[0:P, :])]
-        l6 = load_list(offs6, "l6")
-        so_t = load_bound_step(so, "so_t")
-        l7 = load_list(offs7, "l7")
-        sp_t = load_bound_step(sp, "sp_t")
-        tzs.append(load([P, G], F32, "tz1", tz[P:2 * P, :]))
+        w2_w = load_words(w2_words[0].rearrange("p c t -> p (c t)"), 4 * R, "w2_w")
+        w_w = load_words(w_words[0], 2 * R, "w_w")
         l4 = load_list(offs4, "l4")
         sa_t = load_factor(sa, "sa_t")
         l5 = load_list(offs5, "l5")
         sb_t = load_factor(sb, "sb_t")
         wb_w = load_words(wb_words[0].rearrange("p c t -> p (c t)"), 4 * N, "wb_w")
-        wb_st = stage_scales(wb_scales, N, "wb_st")
+        tzs = [load([P, G], F32, "tz%d" % b, tz[P * b:P * (b + 1), :]) for b in range(N // P)]
+        l6 = load_list(offs6, "l6")
+        so_t = load_bound_step(so, "so_t")
+        l7 = load_list(offs7, "l7")
+        sp_t = load_bound_step(sp, "sp_t")
+        wb_s = sb_tile([P, N], U8, "wb_s")
+        nc.vector.memset(wb_s[:].bitcast(I32), 0)
+        for quad in range(4):
+            nc.sync.dma_start(out=wb_s[32 * quad:32 * quad + 4, :].bitcast(I32),
+                              in_=wb_scales[0, 4 * quad:4 * quad + 4, :].bitcast(I32))
 
         xo_s = spread_scales(xo_st, M, "xo_s")
         xg_w = sb_tile([P, 2 * J], U8, "xg_w")
@@ -118,81 +124,113 @@ def tile_picked_largercode_plain_bank_pooledgroups_one_lastbounds_kernel(tc, ta,
         nc.vector.tensor_copy(out=xg_w[:].bitcast(U16), in_=xo_w[:].bitcast(U16).indirect(l3[:]))
         nc.vector.tensor_copy(out=xg_s[:], in_=xo_s[:].indirect(l3[:]))
 
-        wd_w = sb_tile([P, 2 * R], U8, "wd_w")
-        nc.scalar.copy(out=wd_w[:].bitcast(U16).rearrange("p (t m) -> p t m", t=PACK),
-                       in_=w_w[:].bitcast(U16).rearrange("p (m t) -> p t m", t=PACK))
         wd_s = deal_scales(spread_scales(w_st, R, "w_s"), "wd_s")
-        w2d_w = sb_tile([P, 4 * R], U8, "w2d_w")
-        nc.vector.tensor_copy(out=w2d_w[:].bitcast(I32).rearrange("p (t m) -> p t m", t=PACK),
-                              in_=w2_w[:].bitcast(I32).rearrange("p (m t) -> p t m", t=PACK))
         w2d_s = deal_scales(spread_scales(w2_st, R, "w2_s"), "w2d_s")
 
-        groups = [(0, 0, HALF), (0, HALF, HALF)] + [(t, 0, J) for t in range(1, PACK)]
-        banks = [psum.tile([P, width], F32, name="acc%d" % i) for i, (t, c0, width) in enumerate(groups)]
-        for bank, (t, c0, width) in zip(banks, groups):
+        pairs = [sb_tile([P, 2, CHUNK, 2], BF16, "pairs%d" % c) for c in range(CHUNKS)]
+        xcs = [sb_tile([P, CHUNK * PACK], BF16, "xc%d" % c) for c in range(CHUNKS)]
+        xq_w = sb_tile([P, J], U32, "xq_w")
+        xq_s = sb_tile([P, J], U8, "xq_s")
+        wd_w = sb_tile([P, 2 * R], U8, "wd_w")
+        w2d_w = sb_tile([P, 4 * R], U8, "w2d_w")
+        for t in range(PACK):
+            pa = sb_tile([P, J], F32, "pa%d" % t)
+            pb = sb_tile([P, J], F32, "pb%d" % t)
+            nc.scalar.activation(out=pa[:], in_=tas[t][:].indirect(l1[:]), func=COPY, scale=ga_t[:, t:t + 1])
+            nc.scalar.activation(out=pb[:], in_=tbs[t][:].indirect(l2[:]), func=COPY, scale=gb_t[:, t:t + 1])
+            if t == PACK - 1:
+                nc.vector.tensor_copy(out=w2d_w[:].bitcast(I32).rearrange("p (t m) -> p m t", t=PACK),
+                                      in_=w2_w[:].bitcast(I32).rearrange("p (m t) -> p m t", t=PACK))
+                nc.vector.tensor_copy(out=wd_w[:].bitcast(U16).rearrange("p (t m) -> p m t", t=PACK),
+                                      in_=w_w[:].bitcast(U16).rearrange("p (m t) -> p m t", t=PACK))
+            for c in range(CHUNKS):
+                cols = slice(CHUNK * c, CHUNK * (c + 1))
+                nc.vector.tensor_tensor(out=pairs[c][:, t // 2, :, t % 2], in0=pa[:, cols], in1=pb[:, cols], op=MAX)
+
+        groups = [(0, CHUNK * c, CHUNK) for c in range(CHUNKS)] + [(t, 0, J) for t in range(1, PACK)]
+        banks = [psum.tile([P, width], F32, name="acc%d" % i, tag="acc%d" % i) for i, (t, c0, width) in enumerate(groups)]
+
+        def notes_pass(i):
+            bank = banks[i]
+            t, c0, width = groups[i]
             nc.tensor.matmul_mx(out=bank[:],
                                 lhsT=w2d_w[:, 4 * P * t:4 * P * (t + 1)].bitcast(FP8X4),
                                 lhsT_scale=w2d_s[:, P * t:P * (t + 1)],
                                 rhs=xg_w[:, 2 * c0:2 * (c0 + width)].bitcast(FP4X4),
                                 rhs_scale=xg_s[:, c0:c0 + width], start=True, stop=False)
 
-        xcs = [sb_tile([P, HALF, PACK], BF16, "xc%d" % h) for h in range(2)]
-        xq_w = sb_tile([P, J], U32, "xq_w")
-        xq_s = sb_tile([P, J], U8, "xq_s")
-        for t in range(PACK):
-            pa = sb_tile([P, J], F32, "pa%d" % t)
-            pb = sb_tile([P, J], F32, "pb%d" % t)
-            nc.scalar.activation(out=pa[:], in_=tas[t][:].indirect(l1[:]), func=COPY, scale=ga_t[:, t:t + 1])
-            nc.scalar.activation(out=pb[:], in_=tbs[t][:].indirect(l2[:]), func=COPY, scale=gb_t[:, t:t + 1])
-            for h in range(2):
-                cols = slice(HALF * h, HALF * (h + 1))
-                nc.vector.tensor_tensor(out=xcs[h][:, :, t], in0=pa[:, cols], in1=pb[:, cols], op=MAX)
-        for h in range(2):
-            cols = slice(HALF * h, HALF * (h + 1))
-            nc.vector.quantize_mx(out=xq_w[:, cols].bitcast(FP8X4), scales=xq_s[:, cols],
-                                  in_=xcs[h][:].rearrange("p j t -> p (j t)"))
+        for i in range(CHUNKS):
+            notes_pass(i)
 
-        upper = sb_tile([P, N // P, O], F32, "upper")
-        lower = sb_tile([P, N // P, O], F32, "lower")
-        for b in range(N // P):
-            nc.scalar.activation(out=upper[:, b, :], in_=tzs[b][:].indirect(l6[:]), func=COPY, scale=so_t[:, b:b + 1])
-            nc.scalar.activation(out=lower[:, b, :], in_=tzs[b][:].indirect(l7[:]), func=COPY, scale=sp_t[:, b:b + 1])
+        for c in range(CHUNKS):
+            words_in = pairs[c][:].rearrange("p u j e -> p (u j e)").bitcast(F32).rearrange("p (u j) -> p j u", u=2)
+            words_out = xcs[c][:].bitcast(F32).rearrange("p (j u) -> p j u", u=2)
+            if c < ON_SCALAR:
+                nc.scalar.copy(out=words_out, in_=words_in)
+            else:
+                nc.vector.tensor_copy(out=words_out, in_=words_in)
+        for c in range(CHUNKS):
+            cols = slice(CHUNK * c, CHUNK * (c + 1))
+            nc.vector.quantize_mx(out=xq_w[:, cols].bitcast(FP8X4), scales=xq_s[:, cols], in_=xcs[c][:])
 
-        hidden = [sb_tile([P, J], F32, "hidden%d" % t) for t in range(PACK)]
+        hidden = [keep.tile([P, J], F32, name="hidden%d" % t, tag="hidden%d" % t, align_bytes=64) for t in range(PACK)]
         for i, (bank, (t, c0, width)) in enumerate(zip(banks, groups)):
+            if t > 0:
+                notes_pass(i)
             nc.tensor.matmul_mx(out=bank[:],
                                 lhsT=wd_w[:, 2 * P * t:2 * P * (t + 1)].bitcast(FP4X4),
                                 lhsT_scale=wd_s[:, P * t:P * (t + 1)],
                                 rhs=xq_w[:, c0:c0 + width].bitcast(FP8X4),
                                 rhs_scale=xq_s[:, c0:c0 + width], start=False, stop=True)
-            if i == 0:
+            if t == 0:
                 nc.scalar.copy(out=hidden[t][:, c0:c0 + width], in_=bank[:])
             else:
                 nc.vector.tensor_copy(out=hidden[t][:, c0:c0 + width], in_=bank[:])
 
-        wb_s = spread_scales(wb_st, N, "wb_s")
-
-        hid = sb_tile([P, O, PACK], BF16, "hid")
-        for t in range(PACK):
-            picks = sb_tile([P, 2, S], F32, "picks%d" % t)
-            nc.scalar.activation(out=picks[:, 0, :], in_=hidden[t][:].indirect(l4[:]), func=COPY, scale=sa_t[:, t:t + 1])
-            nc.scalar.activation(out=picks[:, 1, :], in_=hidden[t][:].indirect(l5[:]), func=COPY, scale=sb_t[:, t:t + 1])
-            nc.vector.tensor_reduce(out=hid[:, :, t], in_=picks[:].rearrange("p u (o e) -> p o u e", e=2), axis=XY, op=MAX)
-
+        hids = [sb_tile([P, POOLS, PACK], BF16, "hid%d" % h) for h in range(2)]
         hq_w = sb_tile([P, O], U32, "hq_w")
         hq_s = sb_tile([P, O], U8, "hq_s")
-        nc.vector.quantize_mx(out=hq_w[:].bitcast(FP8X4), scales=hq_s[:], in_=hid[:].rearrange("p o t -> p (o t)"))
 
-        prods = [psum.tile([P, O], F32, name="prod%d" % b) for b in range(N // P)]
-        capped = [sb_tile([P, O], F32, "capped%d" % b) for b in range(N // P)]
-        result = [sb_tile([P, O], F32, "result%d" % b) for b in range(N // P)]
-        for b in range(N // P):
-            nc.tensor.matmul_mx(out=prods[b][:],
-                                lhsT=wb_w[:, 4 * P * b:4 * P * (b + 1)].bitcast(FP8X4),
-                                lhsT_scale=wb_s[:, P * b:P * (b + 1)],
-                                rhs=hq_w[:].bitcast(FP8X4), rhs_scale=hq_s[:], start=True, stop=True)
-        for b in range(N // P):
-            nc.vector.tensor_tensor(out=capped[b][:], in0=prods[b][:], in1=upper[:, b, :], op=MIN)
-        for b in range(N // P):
-            nc.vector.tensor_tensor(out=result[b][:], in0=capped[b][:], in1=lower[:, b, :], op=MAX)
-            nc.sync.dma_start(out=out[P * b:P * (b + 1), :], in_=result[b][:])
+        def pick(t, s0, n):
+            picks = sb_tile([P, 2, n], F32, "picks%d_%d" % (t, s0))
+            lcols = slice(s0 // 16, (s0 + n) // 16)
+            nc.scalar.activation(out=picks[:, 0, :], in_=hidden[t][:].indirect(l4[:, lcols]), func=COPY, scale=sa_t[:, t:t + 1])
+            nc.scalar.activation(out=picks[:, 1, :], in_=hidden[t][:].indirect(l5[:, lcols]), func=COPY, scale=sb_t[:, t:t + 1])
+            return picks
+
+        def pool(t, h, picks):
+            nc.vector.tensor_reduce(out=hids[h][:, :, t], in_=picks.rearrange("p u (o e) -> p o u e", e=2), axis=XY, op=MAX)
+
+        for t in range(PACK - 1):
+            picks = pick(t, 0, S)
+            for h in range(2):
+                pool(t, h, picks[:, :, 2 * POOLS * h:2 * POOLS * (h + 1)])
+        prods = []
+        for h in range(2):
+            pool(PACK - 1, h, pick(PACK - 1, 2 * POOLS * h, 2 * POOLS)[:])
+            cols = slice(POOLS * h, POOLS * (h + 1))
+            nc.vector.quantize_mx(out=hq_w[:, cols].bitcast(FP8X4), scales=hq_s[:, cols],
+                                  in_=hids[h][:].rearrange("p o t -> p (o t)"))
+            prod = psum.tile([P, N // P, POOLS], F32, name="prod%d" % h, tag="acc%d" % h)
+            for b in range(N // P):
+                nc.tensor.matmul_mx(out=prod[:, b, :],
+                                    lhsT=wb_w[:, 4 * P * b:4 * P * (b + 1)].bitcast(FP8X4),
+                                    lhsT_scale=wb_s[:, P * b:P * (b + 1)],
+                                    rhs=hq_w[:, cols].bitcast(FP8X4), rhs_scale=hq_s[:, cols], start=True, stop=True)
+            prods.append(prod)
+
+        bounds = keep.tile([P, 2, N // P, O], F32, name="bounds", tag="hidden%d" % (PACK - 1), align_bytes=64)
+        for u, (lst, step) in enumerate(((l6, so_t), (l7, sp_t))):
+            for b in range(N // P):
+                nc.scalar.activation(out=bounds[:, u, b, :], in_=tzs[b][:].indirect(lst[:]), func=COPY, scale=step[:, b:b + 1])
+
+        capped = [sb_tile([P, N // P, POOLS], F32, "capped%d" % h) for h in range(2)]
+        result = sb_tile([P, N // P, O], F32, "result")
+        for h in range(2):
+            cols = slice(POOLS * h, POOLS * (h + 1))
+            nc.vector.tensor_tensor(out=capped[h][:], in0=prods[h][:], in1=bounds[:, 0, :, cols], op=MIN)
+        for h in range(2):
+            cols = slice(POOLS * h, POOLS * (h + 1))
+            nc.vector.tensor_tensor(out=result[:, :, cols], in0=capped[h][:], in1=bounds[:, 1, :, cols], op=MAX)
+        nc.sync.dma_start(out=out[0:P, :], in_=result[:, 0, :])
+        nc.scalar.dma_start(out=out[P:2 * P, :], in_=result[:, 1, :])

@@ -23,6 +23,7 @@ PACK = 4
 CHUNK = 128
 CHUNKS = J // CHUNK
 ON_SCALAR = 2
+ORDER = (2, 3, 0, 1)
 POOLS = O // 2
 
 
@@ -63,8 +64,8 @@ def tile_picked_largercode_plain_bank_pooledgroups_one_lastbounds_kernel(tc, ta,
 
         def stage_scales(src, cols, name):
             t = sb_tile([P, 2, cols], U8, name)
-            for u in range(2):
-                nc.sync.dma_start(out=t[64 * u:64 * u + 4].bitcast(I32),
+            for u, queue in enumerate((nc.sync, nc.scalar)):
+                queue.dma_start(out=t[64 * u:64 * u + 4].bitcast(I32),
                                   in_=src[0, 8 * u:8 * u + 8, :].rearrange("(q i) c -> i q c", i=4).bitcast(I32))
             return t
 
@@ -141,18 +142,20 @@ def tile_picked_largercode_plain_bank_pooledgroups_one_lastbounds_kernel(tc, ta,
             if t == PACK - 1:
                 nc.vector.tensor_copy(out=w2d_w[:].bitcast(I32).rearrange("p (t m) -> p m t", t=PACK),
                                       in_=w2_w[:].bitcast(I32).rearrange("p (m t) -> p m t", t=PACK))
-                nc.vector.tensor_copy(out=wd_w[:].bitcast(U16).rearrange("p (t m) -> p m t", t=PACK),
+                nc.scalar.copy(out=wd_w[:].bitcast(U16).rearrange("p (t m) -> p m t", t=PACK),
                                       in_=w_w[:].bitcast(U16).rearrange("p (m t) -> p m t", t=PACK))
             for c in range(CHUNKS):
                 cols = slice(CHUNK * c, CHUNK * (c + 1))
                 nc.vector.tensor_tensor(out=pairs[c][:, t // 2, :, t % 2], in0=pa[:, cols], in1=pb[:, cols], op=MAX)
 
-        groups = [(0, CHUNK * c, CHUNK) for c in range(CHUNKS)] + [(t, 0, J) for t in range(1, PACK)]
-        banks = [psum.tile([P, width], F32, name="acc%d" % i, tag="acc%d" % i) for i, (t, c0, width) in enumerate(groups)]
+        groups = [(0, CHUNK * c, CHUNK) for c in ORDER] + [(t, 0, J) for t in range(1, PACK)]
+        tags = ["acc0", "acc1", "acc2", "acc3", "acc4", "acc2", "acc3"]
+        banks = {}
 
         def notes_pass(i):
-            bank = banks[i]
             t, c0, width = groups[i]
+            bank = psum.tile([P, width], F32, name="acc%d" % i, tag=tags[i])
+            banks[i] = bank
             nc.tensor.matmul_mx(out=bank[:],
                                 lhsT=w2d_w[:, 4 * P * t:4 * P * (t + 1)].bitcast(FP8X4),
                                 lhsT_scale=w2d_s[:, P * t:P * (t + 1)],
@@ -169,14 +172,15 @@ def tile_picked_largercode_plain_bank_pooledgroups_one_lastbounds_kernel(tc, ta,
                 nc.scalar.copy(out=words_out, in_=words_in)
             else:
                 nc.vector.tensor_copy(out=words_out, in_=words_in)
-        for c in range(CHUNKS):
+        for c in ORDER:
             cols = slice(CHUNK * c, CHUNK * (c + 1))
             nc.vector.quantize_mx(out=xq_w[:, cols].bitcast(FP8X4), scales=xq_s[:, cols], in_=xcs[c][:])
 
         hidden = [keep.tile([P, J], F32, name="hidden%d" % t, tag="hidden%d" % t, align_bytes=64) for t in range(PACK)]
-        for i, (bank, (t, c0, width)) in enumerate(zip(banks, groups)):
+        for i, (t, c0, width) in enumerate(groups):
             if t > 0:
                 notes_pass(i)
+            bank = banks[i]
             nc.tensor.matmul_mx(out=bank[:],
                                 lhsT=wd_w[:, 2 * P * t:2 * P * (t + 1)].bitcast(FP4X4),
                                 lhsT_scale=wd_s[:, P * t:P * (t + 1)],

@@ -20,14 +20,20 @@ XY = mybir.AxisListType.XY
 
 P = 128
 PACK = 4
+FP8_BYTES, FP4_BYTES = 4, 2
+LIST_ROWS = 16
+QUADS, QUAD_ROWS, SCALE_ROWS = 4, 32, 4
+BLOCKS = N // P
 CHUNK = 128
 CHUNKS = J // CHUNK
 ON_SCALAR = 2
-ORDER = (2, 3, 0, 1)
-POOLS = O // 2
+CHUNK_ORDER = tuple(range(ON_SCALAR, CHUNKS)) + tuple(range(ON_SCALAR))
+HALVES = 2
+POOLS = O // HALVES
 
 
-def tile_picked_largercode_plain_bank_pooledgroups_one_lastbounds_kernel(tc, ta, tb, ga, gb, w_words, w_scales, xo_words, xo_scales, w2_words, w2_scales,
+def tile_picked_largercode_plain_bank_pooledgroups_one_lastbounds_kernel(
+        tc, ta, tb, ga, gb, w_words, w_scales, xo_words, xo_scales, w2_words, w2_scales,
         sa, sb, wb_words, wb_scales, tz, so, sp, offs, offs2, offs3, offs4, offs5, offs6, offs7, out):
     nc = tc.nc
     with ExitStack() as ctx:
@@ -38,9 +44,9 @@ def tile_picked_largercode_plain_bank_pooledgroups_one_lastbounds_kernel(tc, ta,
             return keep.tile(shape, dtype, name=name, align_bytes=64)
 
         def load(shape, dtype, name, src):
-            t = sb_tile(shape, dtype, name)
-            nc.sync.dma_start(out=t[:], in_=src)
-            return t
+            dst = sb_tile(shape, dtype, name)
+            nc.sync.dma_start(out=dst[:], in_=src)
+            return dst
 
         def load_table(src, t, name):
             return load([P, T], F32, name + str(t), src.rearrange("(p t) c -> t p c", t=PACK)[t])
@@ -52,36 +58,39 @@ def tile_picked_largercode_plain_bank_pooledgroups_one_lastbounds_kernel(tc, ta,
             return load([P, PACK], F32, name, src.rearrange("(p t) o -> p (t o)", t=PACK))
 
         def load_bound_step(src, name):
-            t = sb_tile([P, N // P], F32, name)
+            dst = sb_tile([P, BLOCKS], F32, name)
             with nc.allow_non_contiguous_dma(reason="one value a partition and block"):
-                nc.sync.dma_start(out=t[:], in_=src.rearrange("(b p) o -> p (b o)", p=P))
-            return t
+                nc.sync.dma_start(out=dst[:], in_=src.rearrange("(b p) o -> p (b o)", p=P))
+            return dst
 
         def load_words(src, nbytes, name):
-            t = sb_tile([P, nbytes], U8, name)
-            nc.sync.dma_start(out=t[:].bitcast(I32), in_=src.bitcast(I32))
-            return t
+            dst = sb_tile([P, nbytes], U8, name)
+            nc.sync.dma_start(out=dst[:].bitcast(I32), in_=src.bitcast(I32))
+            return dst
 
         def stage_scales(src, cols, name):
-            t = sb_tile([P, 2, cols], U8, name)
+            stage = sb_tile([P, 2, cols], U8, name)
             for u, queue in enumerate((nc.sync, nc.scalar)):
-                queue.dma_start(out=t[64 * u:64 * u + 4].bitcast(I32),
-                                  in_=src[0, 8 * u:8 * u + 8, :].rearrange("(q i) c -> i q c", i=4).bitcast(I32))
-            return t
+                rows = src[0, 2 * SCALE_ROWS * u:2 * SCALE_ROWS * (u + 1), :]
+                queue.dma_start(out=stage[2 * QUAD_ROWS * u:2 * QUAD_ROWS * u + SCALE_ROWS].bitcast(I32),
+                                in_=rows.rearrange("(q i) c -> i q c", i=SCALE_ROWS).bitcast(I32))
+            return stage
 
         def spread_scales(stage, cols, name):
-            plane = sb_tile([P, cols], U8, name)
-            nc.vector.memset(plane[:].bitcast(I32), 0)
-            for quad in range(4):
+            rows = sb_tile([P, cols], U8, name)
+            nc.vector.memset(rows[:].bitcast(I32), 0)
+            for quad in range(QUADS):
                 u, q = divmod(quad, 2)
-                nc.vector.tensor_copy(out=plane[32 * quad:32 * quad + 4, :].bitcast(I32),
-                                      in_=stage[64 * u:64 * u + 4, q, :].bitcast(I32))
-            return plane
+                nc.vector.tensor_copy(out=rows[QUAD_ROWS * quad:QUAD_ROWS * quad + SCALE_ROWS, :].bitcast(I32),
+                                      in_=stage[2 * QUAD_ROWS * u:2 * QUAD_ROWS * u + SCALE_ROWS, q, :].bitcast(I32))
+            return rows
 
-        def deal_scales(plane, name):
+        def deal(copy, dst, src):
+            copy(out=dst.rearrange("p (t m) -> p m t", t=PACK), in_=src.rearrange("p (m t) -> p m t", t=PACK))
+
+        def deal_scales(rows, name):
             dealt = sb_tile([P, R], U8, name)
-            nc.vector.tensor_copy(out=dealt[:].rearrange("p (t m) -> p m t", t=PACK),
-                                  in_=plane[:].rearrange("p (m t) -> p m t", t=PACK))
+            deal(nc.vector.tensor_copy, dealt[:], rows[:])
             return dealt
 
         xo_st = stage_scales(xo_scales, M, "xo_st")
@@ -96,31 +105,31 @@ def tile_picked_largercode_plain_bank_pooledgroups_one_lastbounds_kernel(tc, ta,
         gb_t = load_factor(gb, "gb_t")
         tas.append(load_table(ta, 1, "ta"))
         l3 = load_list(offs3, "l3")
-        xo_w = load_words(xo_words[0], 2 * M, "xo_w")
+        xo_w = load_words(xo_words[0], FP4_BYTES * M, "xo_w")
         tbs.append(load_table(tb, 1, "tb"))
-        for t in (2, 3):
+        for t in range(2, PACK):
             tas.append(load_table(ta, t, "ta"))
             tbs.append(load_table(tb, t, "tb"))
-        w2_w = load_words(w2_words[0].rearrange("p c t -> p (c t)"), 4 * R, "w2_w")
-        w_w = load_words(w_words[0], 2 * R, "w_w")
+        w2_w = load_words(w2_words[0].rearrange("p c t -> p (c t)"), FP8_BYTES * R, "w2_w")
+        w_w = load_words(w_words[0], FP4_BYTES * R, "w_w")
         l4 = load_list(offs4, "l4")
         sa_t = load_factor(sa, "sa_t")
         l5 = load_list(offs5, "l5")
         sb_t = load_factor(sb, "sb_t")
-        wb_w = load_words(wb_words[0].rearrange("p c t -> p (c t)"), 4 * N, "wb_w")
-        tzs = [load([P, G], F32, "tz%d" % b, tz[P * b:P * (b + 1), :]) for b in range(N // P)]
+        wb_w = load_words(wb_words[0].rearrange("p c t -> p (c t)"), FP8_BYTES * N, "wb_w")
+        tzs = [load([P, G], F32, "tz%d" % b, tz[P * b:P * (b + 1), :]) for b in range(BLOCKS)]
         l6 = load_list(offs6, "l6")
         so_t = load_bound_step(so, "so_t")
         l7 = load_list(offs7, "l7")
         sp_t = load_bound_step(sp, "sp_t")
         wb_s = sb_tile([P, N], U8, "wb_s")
         nc.vector.memset(wb_s[:].bitcast(I32), 0)
-        for quad in range(4):
-            nc.sync.dma_start(out=wb_s[32 * quad:32 * quad + 4, :].bitcast(I32),
-                              in_=wb_scales[0, 4 * quad:4 * quad + 4, :].bitcast(I32))
+        for quad in range(QUADS):
+            nc.sync.dma_start(out=wb_s[QUAD_ROWS * quad:QUAD_ROWS * quad + SCALE_ROWS, :].bitcast(I32),
+                              in_=wb_scales[0, SCALE_ROWS * quad:SCALE_ROWS * (quad + 1), :].bitcast(I32))
 
         xo_s = spread_scales(xo_st, M, "xo_s")
-        xg_w = sb_tile([P, 2 * J], U8, "xg_w")
+        xg_w = sb_tile([P, FP4_BYTES * J], U8, "xg_w")
         xg_s = sb_tile([P, J], U8, "xg_s")
         nc.vector.tensor_copy(out=xg_w[:].bitcast(U16), in_=xo_w[:].bitcast(U16).indirect(l3[:]))
         nc.vector.tensor_copy(out=xg_s[:], in_=xo_s[:].indirect(l3[:]))
@@ -132,34 +141,31 @@ def tile_picked_largercode_plain_bank_pooledgroups_one_lastbounds_kernel(tc, ta,
         xcs = [sb_tile([P, CHUNK * PACK], BF16, "xc%d" % c) for c in range(CHUNKS)]
         xq_w = sb_tile([P, J], U32, "xq_w")
         xq_s = sb_tile([P, J], U8, "xq_s")
-        wd_w = sb_tile([P, 2 * R], U8, "wd_w")
-        w2d_w = sb_tile([P, 4 * R], U8, "w2d_w")
+        wd_w = sb_tile([P, FP4_BYTES * R], U8, "wd_w")
+        w2d_w = sb_tile([P, FP8_BYTES * R], U8, "w2d_w")
         for t in range(PACK):
             pa = sb_tile([P, J], F32, "pa%d" % t)
             pb = sb_tile([P, J], F32, "pb%d" % t)
             nc.scalar.activation(out=pa[:], in_=tas[t][:].indirect(l1[:]), func=COPY, scale=ga_t[:, t:t + 1])
             nc.scalar.activation(out=pb[:], in_=tbs[t][:].indirect(l2[:]), func=COPY, scale=gb_t[:, t:t + 1])
             if t == PACK - 1:
-                nc.vector.tensor_copy(out=w2d_w[:].bitcast(I32).rearrange("p (t m) -> p m t", t=PACK),
-                                      in_=w2_w[:].bitcast(I32).rearrange("p (m t) -> p m t", t=PACK))
-                nc.scalar.copy(out=wd_w[:].bitcast(U16).rearrange("p (t m) -> p m t", t=PACK),
-                                      in_=w_w[:].bitcast(U16).rearrange("p (m t) -> p m t", t=PACK))
+                deal(nc.vector.tensor_copy, w2d_w[:].bitcast(I32), w2_w[:].bitcast(I32))
+                deal(nc.scalar.copy, wd_w[:].bitcast(U16), w_w[:].bitcast(U16))
             for c in range(CHUNKS):
                 cols = slice(CHUNK * c, CHUNK * (c + 1))
                 nc.vector.tensor_tensor(out=pairs[c][:, t // 2, :, t % 2], in0=pa[:, cols], in1=pb[:, cols], op=MAX)
 
-        groups = [(0, CHUNK * c, CHUNK) for c in ORDER] + [(t, 0, J) for t in range(1, PACK)]
-        tags = ["acc0", "acc1", "acc2", "acc3", "acc4", "acc2", "acc3"]
+        groups = [(0, CHUNK * c, CHUNK) for c in CHUNK_ORDER] + [(t, 0, J) for t in range(1, PACK)]
+        tags = ["acc%d" % i for i in range(len(groups) - 1)] + ["acc%d" % (CHUNKS - 1)]
         banks = {}
 
         def notes_pass(i):
             t, c0, width = groups[i]
-            bank = psum.tile([P, width], F32, name="acc%d" % i, tag=tags[i])
-            banks[i] = bank
-            nc.tensor.matmul_mx(out=bank[:],
-                                lhsT=w2d_w[:, 4 * P * t:4 * P * (t + 1)].bitcast(FP8X4),
+            banks[i] = psum.tile([P, width], F32, name="acc%d" % i, tag=tags[i])
+            nc.tensor.matmul_mx(out=banks[i][:],
+                                lhsT=w2d_w[:, FP8_BYTES * P * t:FP8_BYTES * P * (t + 1)].bitcast(FP8X4),
                                 lhsT_scale=w2d_s[:, P * t:P * (t + 1)],
-                                rhs=xg_w[:, 2 * c0:2 * (c0 + width)].bitcast(FP4X4),
+                                rhs=xg_w[:, FP4_BYTES * c0:FP4_BYTES * (c0 + width)].bitcast(FP4X4),
                                 rhs_scale=xg_s[:, c0:c0 + width], start=True, stop=False)
 
         for i in range(CHUNKS):
@@ -172,7 +178,7 @@ def tile_picked_largercode_plain_bank_pooledgroups_one_lastbounds_kernel(tc, ta,
                 nc.scalar.copy(out=words_out, in_=words_in)
             else:
                 nc.vector.tensor_copy(out=words_out, in_=words_in)
-        for c in ORDER:
+        for c in CHUNK_ORDER:
             cols = slice(CHUNK * c, CHUNK * (c + 1))
             nc.vector.quantize_mx(out=xq_w[:, cols].bitcast(FP8X4), scales=xq_s[:, cols], in_=xcs[c][:])
 
@@ -180,61 +186,64 @@ def tile_picked_largercode_plain_bank_pooledgroups_one_lastbounds_kernel(tc, ta,
         for i, (t, c0, width) in enumerate(groups):
             if t > 0:
                 notes_pass(i)
-            bank = banks[i]
-            nc.tensor.matmul_mx(out=bank[:],
-                                lhsT=wd_w[:, 2 * P * t:2 * P * (t + 1)].bitcast(FP4X4),
+            nc.tensor.matmul_mx(out=banks[i][:],
+                                lhsT=wd_w[:, FP4_BYTES * P * t:FP4_BYTES * P * (t + 1)].bitcast(FP4X4),
                                 lhsT_scale=wd_s[:, P * t:P * (t + 1)],
                                 rhs=xq_w[:, c0:c0 + width].bitcast(FP8X4),
                                 rhs_scale=xq_s[:, c0:c0 + width], start=False, stop=True)
             if t == 0:
-                nc.scalar.copy(out=hidden[t][:, c0:c0 + width], in_=bank[:])
+                nc.scalar.copy(out=hidden[t][:, c0:c0 + width], in_=banks[i][:])
             else:
-                nc.vector.tensor_copy(out=hidden[t][:, c0:c0 + width], in_=bank[:])
+                nc.vector.tensor_copy(out=hidden[t][:, c0:c0 + width], in_=banks[i][:])
 
-        hids = [sb_tile([P, POOLS, PACK], BF16, "hid%d" % h) for h in range(2)]
+        hids = [sb_tile([P, POOLS, PACK], BF16, "hid%d" % h) for h in range(HALVES)]
         hq_w = sb_tile([P, O], U32, "hq_w")
         hq_s = sb_tile([P, O], U8, "hq_s")
 
-        def pick(t, s0, n):
-            picks = sb_tile([P, 2, n], F32, "picks%d_%d" % (t, s0))
-            lcols = slice(s0 // 16, (s0 + n) // 16)
-            nc.scalar.activation(out=picks[:, 0, :], in_=hidden[t][:].indirect(l4[:, lcols]), func=COPY, scale=sa_t[:, t:t + 1])
-            nc.scalar.activation(out=picks[:, 1, :], in_=hidden[t][:].indirect(l5[:, lcols]), func=COPY, scale=sb_t[:, t:t + 1])
+        def pick(t, s0, count):
+            picks = sb_tile([P, 2, count], F32, "picks%d_%d" % (t, s0))
+            entries = slice(s0 // LIST_ROWS, (s0 + count) // LIST_ROWS)
+            nc.scalar.activation(out=picks[:, 0, :], in_=hidden[t][:].indirect(l4[:, entries]), func=COPY,
+                                 scale=sa_t[:, t:t + 1])
+            nc.scalar.activation(out=picks[:, 1, :], in_=hidden[t][:].indirect(l5[:, entries]), func=COPY,
+                                 scale=sb_t[:, t:t + 1])
             return picks
 
-        def pool(t, h, picks):
-            nc.vector.tensor_reduce(out=hids[h][:, :, t], in_=picks.rearrange("p u (o e) -> p o u e", e=2), axis=XY, op=MAX)
+        def largest(t, h, picks):
+            nc.vector.tensor_reduce(out=hids[h][:, :, t], in_=picks.rearrange("p u (o e) -> p o u e", e=2),
+                                    axis=XY, op=MAX)
 
         for t in range(PACK - 1):
             picks = pick(t, 0, S)
-            for h in range(2):
-                pool(t, h, picks[:, :, 2 * POOLS * h:2 * POOLS * (h + 1)])
+            for h in range(HALVES):
+                largest(t, h, picks[:, :, 2 * POOLS * h:2 * POOLS * (h + 1)])
         prods = []
-        for h in range(2):
-            pool(PACK - 1, h, pick(PACK - 1, 2 * POOLS * h, 2 * POOLS)[:])
+        for h in range(HALVES):
+            largest(PACK - 1, h, pick(PACK - 1, 2 * POOLS * h, 2 * POOLS)[:])
             cols = slice(POOLS * h, POOLS * (h + 1))
             nc.vector.quantize_mx(out=hq_w[:, cols].bitcast(FP8X4), scales=hq_s[:, cols],
                                   in_=hids[h][:].rearrange("p o t -> p (o t)"))
-            prod = psum.tile([P, N // P, POOLS], F32, name="prod%d" % h, tag="acc%d" % h)
-            for b in range(N // P):
+            prod = psum.tile([P, BLOCKS, POOLS], F32, name="prod%d" % h, tag=tags[h])
+            for b in range(BLOCKS):
                 nc.tensor.matmul_mx(out=prod[:, b, :],
-                                    lhsT=wb_w[:, 4 * P * b:4 * P * (b + 1)].bitcast(FP8X4),
+                                    lhsT=wb_w[:, FP8_BYTES * P * b:FP8_BYTES * P * (b + 1)].bitcast(FP8X4),
                                     lhsT_scale=wb_s[:, P * b:P * (b + 1)],
                                     rhs=hq_w[:, cols].bitcast(FP8X4), rhs_scale=hq_s[:, cols], start=True, stop=True)
             prods.append(prod)
 
-        bounds = keep.tile([P, 2, N // P, O], F32, name="bounds", tag="hidden%d" % (PACK - 1), align_bytes=64)
-        for u, (lst, step) in enumerate(((l6, so_t), (l7, sp_t))):
-            for b in range(N // P):
-                nc.scalar.activation(out=bounds[:, u, b, :], in_=tzs[b][:].indirect(lst[:]), func=COPY, scale=step[:, b:b + 1])
+        bounds = keep.tile([P, 2, BLOCKS, O], F32, name="bounds", tag="hidden%d" % (PACK - 1), align_bytes=64)
+        for side, (offsets, step) in enumerate(((l6, so_t), (l7, sp_t))):
+            for b in range(BLOCKS):
+                nc.scalar.activation(out=bounds[:, side, b, :], in_=tzs[b][:].indirect(offsets[:]), func=COPY,
+                                     scale=step[:, b:b + 1])
 
-        capped = [sb_tile([P, N // P, POOLS], F32, "capped%d" % h) for h in range(2)]
-        result = sb_tile([P, N // P, O], F32, "result")
-        for h in range(2):
+        capped = [sb_tile([P, BLOCKS, POOLS], F32, "capped%d" % h) for h in range(HALVES)]
+        result = sb_tile([P, BLOCKS, O], F32, "result")
+        for h in range(HALVES):
             cols = slice(POOLS * h, POOLS * (h + 1))
             nc.vector.tensor_tensor(out=capped[h][:], in0=prods[h][:], in1=bounds[:, 0, :, cols], op=MIN)
-        for h in range(2):
+        for h in range(HALVES):
             cols = slice(POOLS * h, POOLS * (h + 1))
             nc.vector.tensor_tensor(out=result[:, :, cols], in0=capped[h][:], in1=bounds[:, 1, :, cols], op=MAX)
-        nc.sync.dma_start(out=out[0:P, :], in_=result[:, 0, :])
-        nc.scalar.dma_start(out=out[P:2 * P, :], in_=result[:, 1, :])
+        for b, queue in enumerate((nc.sync, nc.scalar)):
+            queue.dma_start(out=out[P * b:P * (b + 1), :], in_=result[:, b, :])

from contextlib import ExitStack

import concourse.mybir as mybir

K, J, R, T, M, S, O, N, G = 512, 512, 512, 2048, 1024, 256, 128, 256, 256
FLOPS = 2 * (2 * K * R * J + R * N * O)

F32 = mybir.dt.float32
BF16 = mybir.dt.bfloat16
I32 = mybir.dt.int32
U32 = mybir.dt.uint32
U16 = mybir.dt.uint16
U8 = mybir.dt.uint8
FP8X4 = mybir.dt.float8_e4m3fn_x4
FP4X4 = mybir.dt.float4_e2m1fn_x4
COPY = mybir.ActivationFunctionType.Copy
MAX = mybir.AluOpType.max
MIN = mybir.AluOpType.min
XY = mybir.AxisListType.XY

P = 128
PACK = 4
FP8_BYTES, FP4_BYTES = 4, 2
LIST_ROWS = 16
QUADS, QUAD_ROWS, SCALE_ROWS = 4, 32, 4
BLOCKS = N // P
CHUNK = 128
CHUNKS = J // CHUNK
ON_SCALAR = 2
CHUNK_ORDER = tuple(range(ON_SCALAR, CHUNKS)) + tuple(range(ON_SCALAR))
HALVES = 2
POOLS = O // HALVES


def tile_picked_largercode_plain_bank_pooledgroups_one_lastbounds_kernel(
        tc, ta, tb, ga, gb, w_words, w_scales, xo_words, xo_scales, w2_words, w2_scales,
        sa, sb, wb_words, wb_scales, tz, so, sp, offs, offs2, offs3, offs4, offs5, offs6, offs7, out):
    nc = tc.nc
    with ExitStack() as ctx:
        keep = ctx.enter_context(tc.tile_pool(name="keep", bufs=1))
        psum = ctx.enter_context(tc.psum_pool(name="psum", bufs=1))

        def sb_tile(shape, dtype, name):
            return keep.tile(shape, dtype, name=name, align_bytes=64)

        def load(shape, dtype, name, src):
            dst = sb_tile(shape, dtype, name)
            nc.sync.dma_start(out=dst[:], in_=src)
            return dst

        def load_table(src, t, name):
            return load([P, T], F32, name + str(t), src.rearrange("(p t) c -> t p c", t=PACK)[t])

        def load_list(src, name):
            return load(list(src.shape), U16, name, src)

        def load_factor(src, name):
            return load([P, PACK], F32, name, src.rearrange("(p t) o -> p (t o)", t=PACK))

        def load_bound_step(src, name):
            dst = sb_tile([P, BLOCKS], F32, name)
            with nc.allow_non_contiguous_dma(reason="one value a partition and block"):
                nc.sync.dma_start(out=dst[:], in_=src.rearrange("(b p) o -> p (b o)", p=P))
            return dst

        def load_words(src, nbytes, name):
            dst = sb_tile([P, nbytes], U8, name)
            nc.sync.dma_start(out=dst[:].bitcast(I32), in_=src.bitcast(I32))
            return dst

        def stage_scales(src, cols, name):
            stage = sb_tile([P, 2, cols], U8, name)
            for u, queue in enumerate((nc.sync, nc.scalar)):
                rows = src[0, 2 * SCALE_ROWS * u:2 * SCALE_ROWS * (u + 1), :]
                queue.dma_start(out=stage[2 * QUAD_ROWS * u:2 * QUAD_ROWS * u + SCALE_ROWS].bitcast(I32),
                                in_=rows.rearrange("(q i) c -> i q c", i=SCALE_ROWS).bitcast(I32))
            return stage

        def spread_scales(stage, cols, name):
            rows = sb_tile([P, cols], U8, name)
            nc.vector.memset(rows[:].bitcast(I32), 0)
            for quad in range(QUADS):
                u, q = divmod(quad, 2)
                nc.vector.tensor_copy(out=rows[QUAD_ROWS * quad:QUAD_ROWS * quad + SCALE_ROWS, :].bitcast(I32),
                                      in_=stage[2 * QUAD_ROWS * u:2 * QUAD_ROWS * u + SCALE_ROWS, q, :].bitcast(I32))
            return rows

        def deal(copy, dst, src):
            copy(out=dst.rearrange("p (t m) -> p m t", t=PACK), in_=src.rearrange("p (m t) -> p m t", t=PACK))

        def deal_scales(rows, name):
            dealt = sb_tile([P, R], U8, name)
            deal(nc.vector.tensor_copy, dealt[:], rows[:])
            return dealt

        xo_st = stage_scales(xo_scales, M, "xo_st")
        w2_st = stage_scales(w2_scales, R, "w2_st")
        w_st = stage_scales(w_scales, R, "w_st")
        tas, tbs = [], []
        tas.append(load_table(ta, 0, "ta"))
        l1 = load_list(offs, "l1")
        ga_t = load_factor(ga, "ga_t")
        tbs.append(load_table(tb, 0, "tb"))
        l2 = load_list(offs2, "l2")
        gb_t = load_factor(gb, "gb_t")
        tas.append(load_table(ta, 1, "ta"))
        l3 = load_list(offs3, "l3")
        xo_w = load_words(xo_words[0], FP4_BYTES * M, "xo_w")
        tbs.append(load_table(tb, 1, "tb"))
        for t in range(2, PACK):
            tas.append(load_table(ta, t, "ta"))
            tbs.append(load_table(tb, t, "tb"))
        w2_w = load_words(w2_words[0].rearrange("p c t -> p (c t)"), FP8_BYTES * R, "w2_w")
        w_w = load_words(w_words[0], FP4_BYTES * R, "w_w")
        l4 = load_list(offs4, "l4")
        sa_t = load_factor(sa, "sa_t")
        l5 = load_list(offs5, "l5")
        sb_t = load_factor(sb, "sb_t")
        wb_w = load_words(wb_words[0].rearrange("p c t -> p (c t)"), FP8_BYTES * N, "wb_w")
        tzs = [load([P, G], F32, "tz%d" % b, tz[P * b:P * (b + 1), :]) for b in range(BLOCKS)]
        l6 = load_list(offs6, "l6")
        so_t = load_bound_step(so, "so_t")
        l7 = load_list(offs7, "l7")
        sp_t = load_bound_step(sp, "sp_t")
        wb_s = sb_tile([P, N], U8, "wb_s")
        nc.vector.memset(wb_s[:].bitcast(I32), 0)
        for quad in range(QUADS):
            nc.sync.dma_start(out=wb_s[QUAD_ROWS * quad:QUAD_ROWS * quad + SCALE_ROWS, :].bitcast(I32),
                              in_=wb_scales[0, SCALE_ROWS * quad:SCALE_ROWS * (quad + 1), :].bitcast(I32))

        xo_s = spread_scales(xo_st, M, "xo_s")
        xg_w = sb_tile([P, FP4_BYTES * J], U8, "xg_w")
        xg_s = sb_tile([P, J], U8, "xg_s")
        nc.vector.tensor_copy(out=xg_w[:].bitcast(U16), in_=xo_w[:].bitcast(U16).indirect(l3[:]))
        nc.vector.tensor_copy(out=xg_s[:], in_=xo_s[:].indirect(l3[:]))

        wd_s = deal_scales(spread_scales(w_st, R, "w_s"), "wd_s")
        w2d_s = deal_scales(spread_scales(w2_st, R, "w2_s"), "w2d_s")

        pairs = [sb_tile([P, 2, CHUNK, 2], BF16, "pairs%d" % c) for c in range(CHUNKS)]
        xcs = [sb_tile([P, CHUNK * PACK], BF16, "xc%d" % c) for c in range(CHUNKS)]
        xq_w = sb_tile([P, J], U32, "xq_w")
        xq_s = sb_tile([P, J], U8, "xq_s")
        wd_w = sb_tile([P, FP4_BYTES * R], U8, "wd_w")
        w2d_w = sb_tile([P, FP8_BYTES * R], U8, "w2d_w")
        for t in range(PACK):
            pa = sb_tile([P, J], F32, "pa%d" % t)
            pb = sb_tile([P, J], F32, "pb%d" % t)
            nc.scalar.activation(out=pa[:], in_=tas[t][:].indirect(l1[:]), func=COPY, scale=ga_t[:, t:t + 1])
            nc.scalar.activation(out=pb[:], in_=tbs[t][:].indirect(l2[:]), func=COPY, scale=gb_t[:, t:t + 1])
            if t == PACK - 1:
                deal(nc.vector.tensor_copy, w2d_w[:].bitcast(I32), w2_w[:].bitcast(I32))
                deal(nc.scalar.copy, wd_w[:].bitcast(U16), w_w[:].bitcast(U16))
            for c in range(CHUNKS):
                cols = slice(CHUNK * c, CHUNK * (c + 1))
                nc.vector.tensor_tensor(out=pairs[c][:, t // 2, :, t % 2], in0=pa[:, cols], in1=pb[:, cols], op=MAX)

        groups = [(0, CHUNK * c, CHUNK) for c in CHUNK_ORDER] + [(t, 0, J) for t in range(1, PACK)]
        tags = ["acc%d" % i for i in range(len(groups) - 1)] + ["acc%d" % (CHUNKS - 1)]
        banks = {}

        def notes_pass(i):
            t, c0, width = groups[i]
            banks[i] = psum.tile([P, width], F32, name="acc%d" % i, tag=tags[i])
            nc.tensor.matmul_mx(out=banks[i][:],
                                lhsT=w2d_w[:, FP8_BYTES * P * t:FP8_BYTES * P * (t + 1)].bitcast(FP8X4),
                                lhsT_scale=w2d_s[:, P * t:P * (t + 1)],
                                rhs=xg_w[:, FP4_BYTES * c0:FP4_BYTES * (c0 + width)].bitcast(FP4X4),
                                rhs_scale=xg_s[:, c0:c0 + width], start=True, stop=False)

        for i in range(CHUNKS):
            notes_pass(i)

        for c in range(CHUNKS):
            words_in = pairs[c][:].rearrange("p u j e -> p (u j e)").bitcast(F32).rearrange("p (u j) -> p j u", u=2)
            words_out = xcs[c][:].bitcast(F32).rearrange("p (j u) -> p j u", u=2)
            if c < ON_SCALAR:
                nc.scalar.copy(out=words_out, in_=words_in)
            else:
                nc.vector.tensor_copy(out=words_out, in_=words_in)
        for c in CHUNK_ORDER:
            cols = slice(CHUNK * c, CHUNK * (c + 1))
            nc.vector.quantize_mx(out=xq_w[:, cols].bitcast(FP8X4), scales=xq_s[:, cols], in_=xcs[c][:])

        hidden = [keep.tile([P, J], F32, name="hidden%d" % t, tag="hidden%d" % t, align_bytes=64) for t in range(PACK)]
        for i, (t, c0, width) in enumerate(groups):
            if t > 0:
                notes_pass(i)
            nc.tensor.matmul_mx(out=banks[i][:],
                                lhsT=wd_w[:, FP4_BYTES * P * t:FP4_BYTES * P * (t + 1)].bitcast(FP4X4),
                                lhsT_scale=wd_s[:, P * t:P * (t + 1)],
                                rhs=xq_w[:, c0:c0 + width].bitcast(FP8X4),
                                rhs_scale=xq_s[:, c0:c0 + width], start=False, stop=True)
            if t == 0:
                nc.scalar.copy(out=hidden[t][:, c0:c0 + width], in_=banks[i][:])
            else:
                nc.vector.tensor_copy(out=hidden[t][:, c0:c0 + width], in_=banks[i][:])

        hids = [sb_tile([P, POOLS, PACK], BF16, "hid%d" % h) for h in range(HALVES)]
        hq_w = sb_tile([P, O], U32, "hq_w")
        hq_s = sb_tile([P, O], U8, "hq_s")

        def pick(t, s0, count):
            picks = sb_tile([P, 2, count], F32, "picks%d_%d" % (t, s0))
            entries = slice(s0 // LIST_ROWS, (s0 + count) // LIST_ROWS)
            nc.scalar.activation(out=picks[:, 0, :], in_=hidden[t][:].indirect(l4[:, entries]), func=COPY,
                                 scale=sa_t[:, t:t + 1])
            nc.scalar.activation(out=picks[:, 1, :], in_=hidden[t][:].indirect(l5[:, entries]), func=COPY,
                                 scale=sb_t[:, t:t + 1])
            return picks

        def largest(t, h, picks):
            nc.vector.tensor_reduce(out=hids[h][:, :, t], in_=picks.rearrange("p u (o e) -> p o u e", e=2),
                                    axis=XY, op=MAX)

        for t in range(PACK - 1):
            picks = pick(t, 0, S)
            for h in range(HALVES):
                largest(t, h, picks[:, :, 2 * POOLS * h:2 * POOLS * (h + 1)])
        prods = []
        for h in range(HALVES):
            largest(PACK - 1, h, pick(PACK - 1, 2 * POOLS * h, 2 * POOLS)[:])
            cols = slice(POOLS * h, POOLS * (h + 1))
            nc.vector.quantize_mx(out=hq_w[:, cols].bitcast(FP8X4), scales=hq_s[:, cols],
                                  in_=hids[h][:].rearrange("p o t -> p (o t)"))
            prod = psum.tile([P, BLOCKS, POOLS], F32, name="prod%d" % h, tag=tags[h])
            for b in range(BLOCKS):
                nc.tensor.matmul_mx(out=prod[:, b, :],
                                    lhsT=wb_w[:, FP8_BYTES * P * b:FP8_BYTES * P * (b + 1)].bitcast(FP8X4),
                                    lhsT_scale=wb_s[:, P * b:P * (b + 1)],
                                    rhs=hq_w[:, cols].bitcast(FP8X4), rhs_scale=hq_s[:, cols], start=True, stop=True)
            prods.append(prod)

        bounds = keep.tile([P, 2, BLOCKS, O], F32, name="bounds", tag="hidden%d" % (PACK - 1), align_bytes=64)
        for side, (offsets, step) in enumerate(((l6, so_t), (l7, sp_t))):
            for b in range(BLOCKS):
                nc.scalar.activation(out=bounds[:, side, b, :], in_=tzs[b][:].indirect(offsets[:]), func=COPY,
                                     scale=step[:, b:b + 1])

        capped = [sb_tile([P, BLOCKS, POOLS], F32, "capped%d" % h) for h in range(HALVES)]
        result = sb_tile([P, BLOCKS, O], F32, "result")
        for h in range(HALVES):
            cols = slice(POOLS * h, POOLS * (h + 1))
            nc.vector.tensor_tensor(out=capped[h][:], in0=prods[h][:], in1=bounds[:, 0, :, cols], op=MIN)
        for h in range(HALVES):
            cols = slice(POOLS * h, POOLS * (h + 1))
            nc.vector.tensor_tensor(out=result[:, :, cols], in0=capped[h][:], in1=bounds[:, 1, :, cols], op=MAX)
        for b, queue in enumerate((nc.sync, nc.scalar)):
            queue.dma_start(out=out[P * b:P * (b + 1), :], in_=result[:, b, :])
